import numpy as np, ml_dtypes
CORES = [40,41,42,43,44,45,46,47]
N = 8
BF = ml_dtypes.bfloat16
H, W, V, K, F, S, R, CAP = 2688, 3072, 2048, 256, 8, 2, 4, 96
def start(q, ans):
    s = np.add.reduce(np.arange(1, 17)[:, None] * q, axis=-2) + ans
    return F * np.arange(K) + (s & (F - 1))
def parts(rng):
    return (rng.integers(0, 256, (N, 8, 16, H)), rng.integers(0, 256, (N, 8, 16, K)), rng.integers(0, H, (N, 8, 16, V)),
            np.ascontiguousarray(np.argsort(rng.random((N, 8, V)), axis=-1)), rng.integers(800, 961, (N, 8)))
def pack(x, q, p, mo, th):
    return {"x": np.ascontiguousarray(x).reshape(N, 128, H).astype(np.float32).astype(BF), "qs": np.ascontiguousarray(q).reshape(N, 128, K).astype(np.float32).astype(BF),
            "towns": np.ascontiguousarray(p).reshape(N, 128, V).astype(np.int32), "mo": np.ascontiguousarray(mo).astype(np.int32),
            "th": np.repeat(th, 16, axis=1).reshape(N, 128, 1).astype(np.int32)}
def mothers(rng, src, dst):
    m = np.zeros(V, np.int64); i = np.arange(V)
    m[src] = dst; m[np.setdiff1d(i, src)] = rng.permutation(np.setdiff1d(i, dst))
    return m
def setup_inputs(rng):
    return pack(*parts(rng))
def setup_inputs_room(rng):
    x, q, p, mo, th = parts(rng)
    x = rng.integers(0, 112, x.shape); th = rng.integers(1, 17, (N, 8))
    for a in range(N):
        for g in range(8):
            n = int(rng.choice(np.array([0, 1, CAP - 1, CAP, CAP + 1, K])))
            if a == 0: n = (CAP, CAP + 1, CAP - 1, 0, 1, K, CAP, K - 1)[g]
            hard = np.zeros(K, bool); hard[rng.permutation(K)[:n]] = True
            rec = rng.integers(0, H - K, K)
            w = np.where(hard, rng.integers(128, 256, (16, K)), x[a, g][:, rec]); w[0, hard] = 128 + 16 * a
            q[a, g] = w; u = start(w, 0)
            e = np.flatnonzero(~hard); p[a, g][rng.integers(0, 8, len(e)), u[e]] = rec[e]
            v = u
            for s in range(S): v = mo[a, g][v]
            b = np.flatnonzero(hard); b = b[rng.random(len(b)) < 0.5]; o = (a + 1) % N
            x[o, g][:, H - K + b] = w[:, b]; p[o, g][rng.integers(8, 16, len(b)), v[b]] = H - K + b
    return pack(x, q, p, mo, th)
def setup_inputs_ties(rng):
    x, q, p, mo, th = parts(rng); o = rng.permutation(8); i, e = o[:4], o[4:]
    x[:, i] = 64 * rng.integers(0, 4, (N, 4, 16, H)); q[:, i] = 64 * rng.integers(0, 4, (N, 4, 16, K))
    y = p[:, i]; y[:, :, 8:, 1::3] = y[:, :, :8, 1::3]; p[:, i] = y
    th[:, i] = rng.choice(np.array([768, 769, 832, 833, 896]), (N, 4))
    k = rng.integers(0, 3, (N, 4, 1, H)); y = np.where(k == 0, 0, np.where(k == 1, 255, x[:, e])); y[..., 0] = 255; x[:, e] = y
    k = rng.integers(0, 3, (N, 4, 1, K)); q[:, e] = np.where(k == 0, 0, np.where(k == 1, 255, q[:, e]))
    y = p[:, e]; y[..., ::5] = 0; p[:, e] = y
    th[:, e] = np.concatenate([rng.permutation(np.array([0, 1, 800, 900, 2000, 4080, 4081, 4096])) for a in range((N + 1) // 2)])[:4 * N].reshape(N, 4)
    return pack(x, q, p, mo, th)
def setup_inputs_alike(rng):
    x, q, p, mo, th = parts(rng)
    pool = rng.integers(0, H, (N, 8, 40)); pool[..., 0] = 0; pool[..., 1] = H - 1
    p = np.take_along_axis(pool, rng.integers(0, 40, (N, 8, 16 * V)), 2).reshape(N, 8, 16, V)
    q[:, :, :, 1::2] = q[:, :, :, 0::2]
    o = rng.permutation(8); i = np.arange(V)
    mo[:, o[0]] = i; mo[:, o[1]] = (i + 1) % V; mo[:, o[2]] = V - 1 - i
    return pack(x, q, p, mo, rng.integers(850, 1001, (N, 8)))
def setup_inputs_crowd(rng):
    x, q, p, mo, th = parts(rng)
    x = rng.integers(0, 96, x.shape); p = rng.integers(0, H - 2 * K, p.shape); th = rng.integers(400, 513, (N, 8))
    for a in range(0, N, 2):
        o = a + 1
        for g in range(8):
            hard = np.zeros(K, bool); hard[rng.permutation(K)[:CAP]] = True
            rec = rng.integers(0, H - 2 * K, K)
            w = x[a, g][:, rec] + rng.integers(0, 8, (16, K)); w[:, hard] = rng.integers(240, 256, (16, CAP))
            q[a, g] = w; u = start(w, 0)
            e = np.flatnonzero(~hard); p[a, g][rng.integers(0, 16, len(e)), u[e]] = rec[e]
            b = np.flatnonzero(hard); c = K * int(rng.integers(0, F))
            free = rng.permutation(np.setdiff1d(np.arange(c, c + K), u[b]))
            way = np.concatenate([u[b], free[:S * CAP]]).reshape(S + 1, CAP)
            mo[a, g] = mothers(rng, way[:-1].reshape(-1), way[1:].reshape(-1))
            x[o, g][:, H - K:H - K + CAP] = 8 * rng.integers(30, 32, (16, CAP))
            p[o, g][rng.integers(8, 16, CAP), way[S]] = H - K + np.arange(CAP)
            x[o, g][:, H - 2 * K:H - K] = rng.integers(136, 200, (16, K))
            if g % 2 == 0: rec = np.full(K, H - 2 * K)
            else:
                rec = H - 2 * K + rng.permutation(K); rec[K - 1] = rec[0]
            w = x[o, g][:, rec] + rng.integers(-8, 9, (16, K))
            q[o, g] = w; u = start(w, 0)
            free = rng.permutation(np.setdiff1d(np.arange(V), u))
            if g // 2 % 2 == 0: free = free[np.argsort(free // K != int(rng.integers(0, F)), kind="stable")]
            v = rng.permutation(free[:K]); mo[o, g] = mothers(rng, u, v)
            p[o, g][rng.integers(0, 8, K), v] = rec
    z = rng.integers(0, H, (N, 8, 1, 1))
    return pack(np.take_along_axis(x, (np.arange(H) - z) % H, 3), q, (p + z) % H, mo, th)
def setup_inputs_spread(rng):
    x, q, p, mo, th = parts(rng)
    x = np.minimum((np.exp2(8.2 * rng.random((N, 8, 1, H))) * rng.random((N, 8, 16, H))).astype(np.int64), 255)
    q = np.minimum((np.exp2(8.2 * rng.random((N, 8, 1, K))) * rng.random((N, 8, 16, K))).astype(np.int64), 255)
    return pack(x, q, p, mo, np.exp2(5 + 6 * rng.random((N, 8))).astype(np.int64))
def check_inputs(d):
    bad = []
    for k in ("x", "qs"):
        v = np.asarray(d[k]).astype(np.float64)
        if not np.all((v >= 0) & (v <= 255) & (v == np.floor(v))): bad.append("whole numbers from 0 to 255 in " + k)
    if np.min(d["towns"]) < 0 or np.max(d["towns"]) > H - 1: bad.append("range of towns")
    m = np.sort(np.asarray(d["mo"]), axis=-1)
    if not np.array_equal(m, np.broadcast_to(np.arange(V), m.shape)): bad.append("the mothers of a group are all different")
    t = np.asarray(d["th"]).reshape(-1, 16)
    if np.min(t) < 0 or np.max(t) > 4096: bad.append("range of th")
    if not np.all(t == t[:, :1]): bad.append("one threshold a group")
    return bad
def tries(rec, lists, u, q, th):
    li = np.take_along_axis(lists, u[:, None, :], 2)
    col = np.take_along_axis(rec, li.reshape(8, 1, 16 * K), 2).reshape(8, 16, 16, K)
    dist = np.add.reduce(np.abs(col - q[:, :, None, :]), axis=1)
    best = np.argmin(dist, axis=1); worst = np.argmax(dist, axis=1)
    num = np.take_along_axis(li, best[:, None, :], 1)[:, 0]
    return np.min(dist, axis=1) < th[:, None], num, worst, li
def reference(x, qs, towns, mo, th):
    X = np.zeros((N, 8, 16, W), np.int32); X[..., :H] = x.astype(np.float32).astype(np.int32).reshape(N, 8, 16, H)
    q = qs.astype(np.float32).astype(np.int32).reshape(N, 8, 16, K)
    P = towns.astype(np.int64).reshape(N, 8, 16, V); M = mo.astype(np.int64); T = th.reshape(N, 8, 16)[:, :, 0].astype(np.int64)
    ans = np.zeros((N, K), np.int64)
    for t in range(R):
        X1, P1, M1, q1, ans1 = X.copy(), P.copy(), M.copy(), q.copy(), ans.copy()
        for a in range(N):
            u = start(q[a].astype(np.int64), ans[a][None, :]); home = np.zeros((8, K), bool); num = np.zeros((8, K), np.int64); path = []
            for s in range(S):
                ok, nm, worst, li = tries(X[a], P[a], u, q[a], T[a])
                hit = ok & ~home; fail = ~ok & ~home
                num = np.where(hit, nm, num); path.append((u, fail, worst, li)); home = home | hit
                u = np.where(fail, np.take_along_axis(M[a], u, 1), u)
            slot = np.add.accumulate((~home).astype(np.int64), axis=1) - 1; place = H + CAP * t + slot
            o = (a + 1 + t) % N
            ok, nm, worst, li = tries(X[o], P[o], u, q[a], T[o])
            came = ok & ~home & (slot < CAP); got = home | came
            old = np.where(home[:, None, :], np.take_along_axis(X[a], num[:, None, :], 2), np.take_along_axis(X[o], nm[:, None, :], 2))
            num = np.where(came, place, num)
            for g in range(8):
                for u_, fail, worst, li in path[::-1]:
                    j = np.flatnonzero(fail[g] & got[g]); new = li[g][:, j]; new[worst[g, j], np.arange(len(j))] = num[g, j]
                    P1[a, g][:, u_[g, j]] = new
                u0, f0 = path[0][0][g], path[0][1][g]
                k = np.flatnonzero(f0[0::2] & f0[1::2]); v, w = u0[2 * k], u0[2 * k + 1]
                M1[a, g, v] = M[a, g, w]; M1[a, g, w] = M[a, g, v]
                j = np.flatnonzero(home[g]); r, i = np.unique(num[g, j], return_index=True); j = j[i]
                X1[a, g][:, r] = (X[a, g][:, r] + q[a, g][:, j]) >> 1
                j = np.flatnonzero(came[g]); X1[a, g][:, place[g, j]] = old[g][:, j]
            q1[a] = np.where(got[:, None, :], (q[a] + old) & 255, q[a])
            ans1[a] = np.add.reduce(got.astype(np.int64), axis=0)
        X, P, M, q, ans = X1, P1, M1, q1, ans1
    return {"yx": X.reshape(N, 128, W).astype(np.float32).astype(BF), "yp": P.reshape(N, 128, V).astype(np.float32), "ym": M.astype(np.float32)}

import numpy as np
from concourse.mybir import dt, AluOpType, ActivationFunctionType

RN, K = 4, 256
OPT = {
    "spath": set(),
    "gvec": set(),
    "qe": 4,
    "reps": True,
    "gs": True,
    "search": 1500, "seed": 3, "bias": {"uXG": -14.8, "ub3": -5.0, "ub4": -5.0, "uB": -8.0},
    "gam": 1.5, "wake": 0.1, "sc": 3.0, "pe": 0.00042, "net": 2.2,
}
F32, BF, I32, U16 = "float32", "bfloat16", "int32", "uint16"
NA, NB = 8, 6
SCRATCH = {}
PACK = {}


def _buf(dtype, **names):
    for nm, n in names.items():
        SCRATCH[nm] = ("sbuf", [128, n], dtype)


def _pack(buf, dtype, **names):
    at = 0
    for nm, n in names.items():
        PACK[nm] = (buf, at, n)
        at += -(-n // 16) * 16
    SCRATCH[buf] = ("sbuf", [128, at], dtype)


_buf(BF, X=3520, XG=4112, Q=256, NQ=256, RQ=1024, REP=272, RP=1152, EXP=2048, ONE=2048, E32=144, EW=144, BO=128, H4=128,
     ID=128, HID=128, CA=128, PSW=128, TB=128, TBx=128, SWx=128, TM=256, KI=256, CQ=256, XH=256, G=256, TQ=256)
_pack("sb", BF, nhb=16, cumb=16, n0b=16, hb=16, hit=32, MK=48)
for _k in range(NA):
    SCRATCH["A%d" % _k] = ("sbuf", [128, 1024], BF)
for _k in range(NB):
    SCRATCH["B%d" % _k] = ("sbuf", [128, 4, 256], BF)
_buf(BF, XC0=1024, XC1=1024, QX=4096)
SCRATCH["EQ"] = ("sbuf", [128, 16, 256], BF)
SCRATCH["TM3"] = ("sbuf", [128, 16, 16], BF)
_buf(F32, P=4096, M=4096, IOT=3232, I256=256, IA=256, IG16=128, BO32=128, ID32=128, NID32=128, MD=256, OH=32, OHW=32,
     RMn=256, RW=256, RS=256, MoF=2048, R8=128, Lf=512, m0=256, SWV=256, GM=256, GS=256,
     SCm=512, SCw=512, SCg=256, WL=512, DGN=256, NS=256, Nf=256, T1=512, T2=512, CM=256, CS=256)
_pack("sf", F32, ONE16=16, IB16=16, IB128=16, cP=1, cA=1, cG=1, cX=1, cT=1, cU=1, cV=1, cW=1, JJ=16, JX=16, JZ=16, th32=1,
      us2=16, pl=16, place=16, numO=16, fst=16, dX=16, dY=16, ry=16, rz=16, pf=16, pz=16, gz=16, gy=16, goy=16, DD=48, YY=48,
      ZZ=48, BS0=48, BS1=48, BS2=48, BS3=48)
_buf(I32, PI=2048, MI=2048, TH=1, RVi=256)
_pack("si", I32, pI=1, pA=1, pB=1, J8=16, GJ=16, sI=16, rI=16, wI=64, wJ=64, gI=16, gJ=16)
_buf(U16, Lu0=256, Lu1=256, LuG=256, RU=64, Nu=256)
_pack("su", U16, U0=16, U1=16, U2=16, GO=16, wU=64, numU=16, roU=16, MOu=16, goU=16, ofU=48)
for _k in range(8):
    SCRATCH["b%d" % _k] = ("psum", [128, 512], F32)
PS = ["b%d" % _k for _k in range(8)]
SEMAPHORES = ["v", "s", "p", "g", "dq", "dx", "dt", "dh", "dm", "o0", "o1", "o2", "o3", "o4"]
SEMAPHORES += [n + str(t) for t in range(RN) for n in ("lq", "rq", "lu", "ru", "lr", "rr")]

ORDER = []
CYC = 0.00083


def _build(g, T, topo, core, rank):
    A, AF = AluOpType, ActivationFunctionType
    V, S, PE = g.vector, g.scalar, g.tensor
    GAM, SC = OPT["gam"], OPT["sc"]
    ops, phase = [], ["s"]

    def C(nm, lo, hi, st=1):
        if nm in PACK:
            nm, at, _ = PACK[nm]
            lo, hi = lo + at, hi + at
        return ([(nm, lo, hi)], T[nm][:, lo:hi:st] if st > 1 else T[nm][:, lo:hi], [])

    def W(nm):
        if nm in PACK:
            return C(nm, 0, PACK[nm][2])
        return ([(nm, 0, 100000)], T[nm][:], [])

    def X3(nm, lo, hi, ap):
        return ([(nm, lo, hi)], ap, [])

    def IX(w, o):
        return (w[0], w[1].indirect(o[1]), o[0])

    def add(q, dur, outs, ins, calls, kind="c", sem=None, inc=1, lat=0.0, dep=None):
        rd, wr = [], []
        for o in ins:
            rd += o[0] + o[2]
        for o in outs:
            wr += o[0]
            rd += o[2]
        nm = wr[0][0] if wr else str(sem)[:2]
        for k, (b, lo, n) in PACK.items():
            if wr and b == nm and lo <= wr[0][1] < lo + n:
                nm = k
                break
        ops.append({"q": q, "dur": dur, "rd": rd, "wr": wr, "calls": calls, "kind": kind, "sem": sem or q, "inc": inc,
                    "lat": lat, "dep": dep, "tag": phase[0] + (nm if nm in PS else nm.rstrip("0123456789"))})
        return len(ops) - 1

    def vc(n, f):
        return 0.05 + CYC * max(64, n * f)

    def copy(o, i, n, f=1.0):
        add("v", vc(n, f), [o], [i], [lambda: V.tensor_copy(o[1], i[1])])

    def tt(o, a, b, op, n, f=2.0):
        add("v", vc(n, f), [o], [a, b], [lambda: V.tensor_tensor(o[1], a[1], b[1], op)])

    def ts(o, i, s1, op0, n, s2=None, op1=None, f=1.0):
        ins = [i] + [s for s in (s1, s2) if isinstance(s, tuple)]
        a1 = s1[1] if isinstance(s1, tuple) else s1
        a2 = s2[1] if isinstance(s2, tuple) else s2
        if op1 is None:
            add("v", vc(n, f), [o], ins, [lambda: V.tensor_scalar(o[1], i[1], a1, None, op0)])
        else:
            add("v", vc(n, f), [o], ins, [lambda: V.tensor_scalar(o[1], i[1], a1, a2, op0, op1)])

    def scan(o, d0, d1, init, op0, op1, n):
        add("v", vc(n, 1), [o], [d0, d1], [lambda: V.tensor_tensor_scan(o[1], d0[1], d1[1], init, op0, op1)])

    def fill(o, c, n):
        add("v", vc(n, 1), [o], [], [lambda: V.memset(o[1], c)])

    def act(o, i, func, n, f=1.0, scale=1.0):
        add("s", 0.065 + CYC * max(64, n * f), [o], [i], [lambda: S.activation(o[1], i[1], func, scale=scale)])

    def mm(o, pairs, start=True, stop=True, f=1):
        calls, ins, dur = [], [], 0.05
        for k, pr in enumerate(pairs):
            l, r, n = pr[:3]
            oo = pr[3] if len(pr) > 3 else o
            ins += [l, r]
            dur += OPT["pe"] * max(64, n) * f + 0.005
            calls.append(lambda l=l, r=r, oo=oo, a=(start and k == 0), z=(stop and k == len(pairs) - 1):
                         PE.matmul(oo[1], l[1], r[1], a, z))
        add("p", dur, [o], ins, calls)

    def iota(o, pat, base, cm, n, flag):
        def f():
            if flag:
                return g.iota(o[1], pat, base, cm, allow_small_or_imprecise_dtypes=True)
            return g.iota(o[1], pat, base, cm)
        add("g", 0.13 + 2 * CYC * n, [o], [], [f])

    def dma(q, sem, o, i, lat, calls=None):
        eng = {"y": g.sync, "s": g.scalar}[q]
        calls = calls or [lambda: eng.dma_start(o[1], i[1])]
        return add(q, 0.1 * len(calls), [o], [i], calls, kind="d", sem=sem, inc=16, lat=lat)

    def send(dst, o, i, ls, rs):
        rid, pid, _ = topo.addr(dst)
        m = topo.mask(core, dst)
        n = len(topo.engines(core, dst))
        k = add("g", 0.8, [], [i], [lambda: g.remote_dma(o[1], i[1], T.sem[rs], T.sem[ls], pid, rid, m)], kind="r", sem=ls,
                inc=n, lat=OPT["net"])
        add(None, 0.0, [o], [], [], kind="w", sem=rs, inc=n, dep=k)

    dma("y", "dq", W("Q"), ([], T.qs[:], []), 2.0)
    dma("y", "dt", W("PI"), ([], T.towns[:], []), 5.0)
    dma("s", "dm", X3("MI", 0, 2048, T.MI[0:8, :]), ([], T.mo[:], []), 2.5)
    dma("s", "dx", C("X", 0, 2688), ([], T.x[:], []), 5.0)
    dma("y", "dh", W("TH"), ([], T.th[:], []), 2.0)
    iota(W("pI"), [[0, 1]], 0, 1, 1, False)
    iota(W("I256"), [[1, 256]], 0, 0, 256, True)
    iota(W("IB128"), [[128, 16]], 0, 0, 16, True)
    iota(W("IA"), [[0, 16], [1, 16]], 0, 0, 256, True)
    iota(W("IG16"), [[16, 8], [0, 16]], 0, 0, 128, True)
    iota(W("IB16"), [[16, 16]], 0, 0, 16, True)
    fill(W("ONE"), 1.0, 2048)
    add("g", 0.17 + 2 * CYC * 2048, [W("EXP")], [W("ONE")],
        [lambda: g.affine_select(T.EXP[:], T.ONE[:], [[-1, 128], [0, 16]], A.is_equal, 0.0, 0, 1)])
    iota(W("IOT"), [[1, 3232]], 0, 0, 3232, True)
    ts(W("pA"), W("pI"), 15, A.bitwise_and, 1)
    ts(W("pB"), W("pI"), 1, A.bitwise_and, 1)
    copy(W("cP"), W("pI"), 1)
    copy(W("cA"), W("pA"), 1)
    tt(W("cG"), W("cP"), W("cA"), A.subtract, 1)
    ts(W("cT"), W("cG"), 15.0, A.add, 1)
    ts(W("cU"), W("cA"), 1.0, A.add, 1)
    ts(W("EW"), C("I256", 0, 144), W("cT"), A.is_equal, 144, W("cU"), A.mult)
    ts(W("cX"), W("cA"), 8.0, A.mult, 1)
    ts(W("J8"), W("IB128"), W("cX"), A.add, 16, 2048.0, A.add)
    ts(W("E32"), C("I256", 0, 144), W("cT"), A.is_equal, 144, 32.0, A.mult)
    ts(W("ID"), C("I256", 0, 128), W("cP"), A.is_equal, 128)
    ts(W("HID"), C("I256", 0, 128), W("cP"), A.is_equal, 128, 0.5, A.mult)
    ts(W("KI"), W("IA"), 2.0, A.mult, 256)
    ts(W("MD"), W("IA"), W("cA"), A.is_equal, 256)
    ts(W("RS"), W("IA"), 0.0, A.not_equal, 256)
    ts(W("th32"), W("TH"), 32.0, A.mult, 1)
    ts(W("R8"), W("IG16"), 0.0625, A.mult, 128)
    ts(W("R8"), W("R8"), W("cP"), A.is_equal, 128)
    ts(W("BO"), W("IG16"), W("cG"), A.is_equal, 128)
    ts(W("BO32"), W("IG16"), W("cG"), A.is_equal, 128)
    ts(W("ID32"), C("I256", 0, 128), W("cP"), A.is_equal, 128)
    ts(W("NID32"), C("I256", 0, 128), W("cP"), A.is_equal, 128, -1.0, A.mult)
    ts(W("H4"), C("I256", 0, 128), W("cP"), A.is_equal, 128, 4096.0, A.mult)
    ts(W("CA"), C("IA", 0, 128), W("cA"), A.is_equal, 128)
    ts(W("cX"), W("pB"), -2.0, A.mult, 1, 1.0, A.add)
    tt(W("cX"), W("cX"), W("cP"), A.add, 1)
    ts(W("SWx"), C("I256", 0, 128), W("cX"), A.is_equal, 128)
    tt(W("PSW"), W("SWx"), W("ID"), A.add, 128)
    ts(W("TBx"), C("IA", 0, 128), W("cA"), A.is_le, 128, -1.0, A.mult)
    tt(W("TB"), W("TBx"), W("BO"), A.mult, 128)
    ts(W("TM"), W("IA"), W("cA"), A.is_gt, 256)
    add("v", 16 * vc(16, 1), [W("TM3")], [W("TM")],
        [lambda b=b: V.tensor_copy(T.TM3[:, b, :], T.TM[:, 16 * b:16 * b + 16]) for b in range(16)])
    ts(W("cV"), W("cA"), 2.0, A.mult, 1, 1.0, A.add)
    ts(W("OH"), C("I256", 0, 32), W("cV"), A.is_equal, 32)
    ts(W("pA"), W("pA"), -2, A.mult, 1, 60, A.add)
    ts(W("pA"), W("pA"), 31, A.bitwise_and, 1)
    copy(W("cW"), W("pA"), 1)
    ts(W("OHW"), C("I256", 0, 32), W("cW"), A.is_equal, 32)
    ts(W("RMn"), W("IA"), 0.0, A.is_equal, 256, 1.0e9, A.mult)
    ts(W("RW"), W("RMn"), -1.0, A.mult, 256, 4.0, A.add)
    fill(W("ONE16"), 1.0, 16)
    fill(W("CQ"), -0.25, 256)
    ts(W("JJ"), W("IB16"), W("cA"), A.add, 16)
    ts(W("JX"), W("JJ"), 3264.0, A.add, 16)
    ts(W("JZ"), W("JJ"), -272.0, A.add, 16)
    ts(W("GJ"), W("JJ"), 16.0, A.mult, 16, -4096.0, A.add)
    fill(C("DD", 0, 32), -2048.0, 32)
    for t in range(RN):
        ts(C("BS%d" % t, 32, 48), W("JJ"), float(576 - 96 * t), A.add, 16)
        fill(C("RP", 288 * t + 272, 288 * t + 288), 0.0, 16)
    fill(C("X", 2688, 3520), 0.0, 832)
    fill(C("XG", 4096, 4112), 0.0, 16)
    copy(C("P", 0, 2048), C("PI", 0, 2048), 2048)
    add("v", vc(2048, 1), [W("MoF")], [W("MI")], [lambda: V.tensor_copy(T.MoF[0:8, :], T.MI[0:8, :])])
    for k in range(4):
        bk = ("b1", "b2", "b3", "b4")[k]
        add("p", 0.9, [W(bk)], [W("R8"), W("MoF")],
            [lambda k=k, bk=bk: PE.matmul(T[bk][:], T.R8[0:8, :], T.MoF[0:8, 512 * k:512 * k + 512], True, True)])
        act(C("M", 512 * k, 512 * k + 512), W(bk), AF.Copy, 512)

    cnt = {"A": 0, "B": 0, "C": 0, "d": 0}

    def ring(kind, n, nm):
        k = cnt[kind] % n
        cnt[kind] += 1
        return nm + str(k)

    def ew(buf):
        return [(C("EW", 15 - a, 143 - a), C(buf, a, 256, 16), 16) for a in range(16)]

    def dsum(key, c, bb):
        pairs = [(W("ID"), C("KI", 64 * c, 64 * c + 64), 64)]
        for a in range(16):
            pairs.append((C("E32", 15 - a, 143 - a), X3(bb, 0, 100000, T[bb][:, :, 16 * a:16 * a + 16]), 64))
        mm(C(key, 64 * c, 64 * c + 64), pairs)

    def expand(nq, n0, k):
        return (C(nq, n0 + 128 * (k // 4), n0 + 128 * (k // 4) + 128), C("EXP", 512 * (k % 4), 512 * (k % 4) + 512), 512)

    def pdiff(xb, x0, nq, n0, c, bb):
        for h in range(2):
            bk = ("b3", "b4")[cnt["d"] % 2]
            cnt["d"] += 1
            mm(W(bk), [(W("ID"), C(xb, x0 + 512 * h, x0 + 512 * h + 512), 512), expand(nq, n0, 2 * c + h)])
            act(X3(bb, 512 * h, 512 * h + 512, T[bb][:, 2 * h:2 * h + 2, :]), W(bk), AF.Abs, 512)

    mm(C("b5", 0, 16), ew("Q"))
    for t in range(RN):
        phase[0] = "a"
        last = t == RN - 1
        to, fro = T.cores[(rank + 1 + t) % 8], T.cores[(rank - 1 - t) % 8]
        Pw, Mw, Xw = C("P", 0, 2048), C("M", 0, 2048), C("X", 0, 3072)
        BS = "BS%d" % t
        copy(W("sI"), C("b5", 0, 16), 16)
        ts(W("rI"), W("sI"), 7, A.bitwise_and, 16)
        tt(C(BS, 0, 16), W("rI"), W("J8"), A.add, 16)
        ts(W("U0"), C(BS, 0, 16), -2048.0, A.add, 16)
        copy(W("Lu0"), IX(Pw, W("U0")), 256, GAM)
        for h in range(2):
            mm(C("b7", 128 * h, 128 * h + 128), [(C("Q", 128 * h, 128 * h + 128), W("ID"), 128)])
        act(W("NQ"), C("b7", 0, 256), AF.Copy, 256, scale=-1.0)
        send(to, C("RQ", 256 * t, 256 * t + 256), W("NQ"), "lq%d" % t, "rq%d" % t)
        if OPT["qe"] is not None:
            for e in range(16):
                o = X3("QX", 4096 * e, 4096 * e + 4096, T.QX[:, e:4096:16])
                if e < OPT["qe"]:
                    copy(o, W("Q"), 256, 0.5)
                else:
                    act(o, W("Q"), AF.Copy, 256)
        else:
            for k in range(8):
                bk = ("b3", "b4")[k % 2]
                mm(W(bk), [expand("NQ", 0, k)])
                act(C("QX", 512 * k, 512 * k + 512), W(bk), AF.Copy, 512, scale=-1.0)
        tt(W("GM"), IX(Mw, W("U0")), W("MD"), A.mult, 256, GAM)
        scan(W("GS"), W("RS"), W("GM"), 0.0, A.mult, A.add, 256)
        copy(W("U1"), C("GS", 15, 256, 16), 16)
        ts(C(BS, 16, 32), C("GS", 15, 256, 16), 2048.0, A.add, 16)
        tt(W("GM"), IX(Mw, W("U1")), W("MD"), A.mult, 256, GAM)
        scan(W("GS"), W("RS"), W("GM"), 0.0, A.mult, A.add, 256)
        copy(W("U2"), C("GS", 15, 256, 16), 16)
        send(to, C("RU", 16 * t, 16 * t + 16), W("U2"), "lu%d" % t, "ru%d" % t)
        copy(W("Lu1"), IX(Pw, W("U1")), 256, GAM)
        copy(W("LuG"), IX(Pw, C("RU", 16 * t, 16 * t + 16)), 256, GAM)
        act(C("Lf", 0, 256), IX(Pw, W("U0")), AF.Copy, 256, GAM)
        act(C("Lf", 256, 512), IX(Pw, W("U1")), AF.Copy, 256, GAM)
        act(W("m0"), IX(Mw, W("U0")), AF.Copy, 256, GAM)
        act(C("SWV", 0, 256, 2), C("m0", 1, 256, 2), AF.Copy, 128)
        act(C("SWV", 1, 256, 2), C("m0", 0, 256, 2), AF.Copy, 128)

        def home(s):
            phase[0] = "h%d" % s
            lu, key = "Lu%d" % s, "b%d" % s
            for c in range(4):
                bb = ring("B", NB, "B")
                ix = IX(Xw, C(lu, 64 * c, 64 * c + 64))
                if (s, c) in OPT["spath"]:
                    xb = ring("C", 2, "XC")
                    act(W(xb), ix, AF.Copy, 1024, GAM)
                    pdiff(xb, 0, "NQ", 0, c, bb)
                else:
                    ab = ring("A", NA, "A")
                    r0, r1 = (1024 * c, 1024 * c + 1024) if OPT["qe"] is None else (0, 65536)
                    tt(W(ab), ix, X3("QX", r0, r1, T.QX[:, 1024 * c:1024 * c + 1024]), A.subtract, 1024, GAM)
                    act(X3(bb, 0, 100000, T[bb][:, :, :]), W(ab), AF.Abs, 1024)
                dsum(key, c, bb)
            scan(C("SCm", 256 * s, 256 * s + 256), W("RMn"), C(key, 0, 256), 0.0, A.max, A.min, 256)
            scan(C("SCw", 256 * s, 256 * s + 256), W("RW"), C(key, 0, 256), 0.0, A.add, A.max, 256)
            ts(C("hit", 16 * s, 16 * s + 16), C("SCm", 256 * s + 15, 256 * s + 256, 16), W("th32"), A.is_lt, 16)

        home(0)
        ts(W("n0b"), C("hit", 0, 16), -1.0, A.mult, 16, 1.0, A.add)
        phase[0] = "u"
        for c in range(4):
            bb = ring("B", NB, "B")
            ix = IX(Xw, C("LuG", 64 * c, 64 * c + 64))
            if c in OPT["gvec"]:
                copy(C("XG", 1024 * c, 1024 * c + 1024), ix, 1024, GAM)
            else:
                act(C("XG", 1024 * c, 1024 * c + 1024), ix, AF.Copy, 1024, GAM)
            pdiff("XG", 1024 * c, "RQ", 256 * t, c, bb)
            dsum("b2", c, bb)
        scan(W("SCg"), W("RMn"), C("b2", 0, 256), 0.0, A.max, A.min, 256)
        gm = C("SCg", 15, 256, 16)
        ts(C("REP", 256, 272), gm, W("th32"), A.is_lt, 16)
        copy(W("gI"), gm, 16)
        ts(W("gJ"), W("gI"), 1, A.logical_shift_right, 16, 15, A.bitwise_and)
        tt(W("gy"), W("gJ"), W("GJ"), A.add, 16)
        tt(W("gz"), W("gy"), C("REP", 256, 272), A.mult, 16)
        ts(W("GO"), W("gz"), 4096.0, A.add, 16)
        ix = IX(C("XG", 0, 4112), W("GO"))
        if OPT["reps"]:
            act(C("REP", 0, 256), ix, AF.Copy, 256, GAM)
        else:
            copy(C("REP", 0, 256), ix, 256, GAM)
        send(fro, C("RP", 288 * t, 288 * t + 272), W("REP"), "lr%d" % t, "rr%d" % t)
        mm(C("b7", 32, 48), [(W("PSW"), W("n0b"), 16)])
        ts(W("pf"), C("b7", 32, 48), 1.5, A.is_ge, 16, -2048.0, A.mult)
        tt(W("pz"), W("pf"), C(BS, 0, 16), A.add, 16)
        copy(W("MOu"), W("pz"), 16)
        copy(IX(C("M", 0, 4096), W("MOu")), W("SWV"), 256, SC)
        home(1)
        phase[0] = "t"
        tt(C("hit", 16, 32), C("hit", 16, 32), W("n0b"), A.mult, 16)
        tt(W("nhb"), W("n0b"), C("hit", 16, 32), A.subtract, 16)
        ts(W("hb"), W("nhb"), -1.0, A.mult, 16, 1.0, A.add)
        tt(C("wI", 0, 32), C("SCm", 15, 512, 16), W("hit"), A.add, 32)
        copy(C("wI", 32, 64), C("SCw", 15, 512, 16), 32)
        ts(W("wJ"), W("wI"), 31, A.bitwise_and, 64)
        copy(W("wU"), W("wJ"), 64)
        tt(W("WL"), IX(W("OH"), C("wU", 0, 32)), W("Lf"), A.mult, 512, GAM)
        mm(C("b6", 0, 256), [(W("BO32"), C("WL", 0, 256), 256), (W("BO32"), C("WL", 256, 512), 256)], f=4)
        tt(W("DGN"), C("b6", 0, 256), W("MD"), A.mult, 256, 1.0)
        scan(W("NS"), W("RS"), W("DGN"), 0.0, A.mult, A.add, 256)
        hn = C("NS", 15, 256, 16)
        scan(W("cumb"), W("ONE16"), W("nhb"), 0.0, A.mult, A.add, 16)
        mm(C("b7", 0, 16), [(W("TB"), W("nhb"), 16), (W("H4"), W("hb"), 16), (W("BO"), W("cumb"), 16)])
        slot = C("b7", 0, 16)
        ts(W("us2"), slot, 96.0, A.is_lt, 16)
        ts(W("pl"), slot, float(2688 + 96 * t), A.add, 16)
        tt(C("DD", 32, 48), slot, C(BS, 32, 48), A.subtract, 16)
        tt(W("place"), W("pl"), W("nhb"), A.mult, 16)
        tt(W("goy"), W("us2"), W("JZ"), A.mult, 16)
        ts(W("goU"), W("goy"), 272.0, A.add, 16)
        tt(W("numO"), hn, W("place"), A.add, 16)
        copy(W("numU"), W("numO"), 16)
        act(W("Nf"), IX(W("IOT"), W("numU")), AF.Copy, 256, GAM)
        act(W("XH"), IX(C("X", 0, 3264), W("numU")), AF.Copy, 256, GAM)
        for s in range(2):
            mm(C("b0", 256 * s, 256 * s + 256), [(W("ID32"), W("Nf"), 256), (W("NID32"), C("Lf", 256 * s, 256 * s + 256), 256)],
               f=4)
        act(W("T1"), W("b0"), AF.Copy, 512)
        tt(W("T2"), IX(W("OHW"), C("wU", 32, 64)), W("T1"), A.mult, 512, GAM)
        tt(W("dX"), hn, W("JX"), A.subtract, 16)
        tt(W("dY"), W("dX"), W("hb"), A.mult, 16)
        copy(W("Nu"), IX(W("IOT"), W("numU")), 256, GAM)
        for b in range(16):
            n = 256 - 16 * b
            ts(X3("EQ", 256 * b, 256 * b + 256, T.EQ[:, b, 0:n]), C("Nu", 16 * b, 256), C("numO", b, b + 1), A.is_equal, n, f=0.5)
        tt(X3("EQ", 0, 4096, T.EQ[:, :, 0:16]), X3("EQ", 0, 4096, T.EQ[:, :, 0:16]), W("TM3"), A.mult, 256)
        mm(C("b7", 0, 256), [(W("BO"), X3("EQ", 256 * b, 256 * b + 256, T.EQ[:, b, 0:256 - 16 * b]), 256 - 16 * b,
                              C("b7", 16 * b, 256)) for b in range(16)])
        tt(W("CM"), C("b7", 0, 256), W("MD"), A.mult, 256, 1.0)
        scan(W("CS"), W("RS"), W("CM"), 0.0, A.mult, A.add, 256)
        ts(W("fst"), C("CS", 15, 256, 16), 0.5, A.is_lt, 16)
        tt(W("ry"), W("fst"), W("dY"), A.mult, 16)
        tt(W("rz"), W("ry"), W("JX"), A.add, 16)
        copy(W("roU"), W("rz"), 16)
        mm(C("b1", 0, 256), [(W("ID"), W("CQ"), 256), (W("HID"), W("Q"), 256), (W("HID"), W("XH"), 256)])
        copy(W("RVi"), C("b1", 0, 256), 256)
        copy(IX(W("X"), W("roU")), W("RVi"), 256, SC)
        RPf = C("RP", 288 * t + 256, 288 * t + 272)
        tt(C("MK", 16, 32), RPf, W("us2"), A.mult, 16)
        tt(C("MK", 32, 48), RPf, W("us2"), A.mult, 16)
        if not last:
            mm(C("b6", 0, 256), [(W("ID"), W("Q"), 256), (W("ID"), W("XH"), 256)], stop=False)
            mm(C("b5", 0, 16), ew("Q") + ew("XH") + [(W("CA"), W("hb"), 16)], stop=False)
            ix = IX(C("RP", 288 * t, 288 * t + 288), W("goU"))
            if OPT["gs"]:
                act(W("G"), ix, AF.Copy, 256, GAM)
            else:
                copy(W("G"), ix, 256, GAM)
            mm(C("b5", 0, 16), [(W("CA"), C("MK", 16, 32), 16)] + ew("G"), start=False)
            mm(C("b6", 0, 256), [(W("ID"), W("G"), 256)], start=False)
            ts(W("TQ"), C("b6", 0, 256), 256.0, A.is_ge, 256, -256.0, A.mult)
            tt(W("Q"), C("b6", 0, 256), W("TQ"), A.add, 256, 1.0)
        tt(C("MK", 0, 16), C("hit", 16, 32), C("MK", 16, 32), A.add, 16)
        tt(W("YY"), W("MK"), W("DD"), A.mult, 48)
        tt(W("ZZ"), W("YY"), W(BS), A.add, 48)
        copy(W("ofU"), W("ZZ"), 48)
        for s in (1, 0):
            tt(IX(W("P"), C("ofU", 16 * s, 16 * s + 16)), C("T2", 256 * s, 256 * s + 256), C("Lf", 256 * s, 256 * s + 256),
               A.add, 256, SC)
        if last:
            dma("y", "o0", ([], T.yx[:, 0:2976], []), C("X", 0, 2976), 5.0)
            dma("y", "o1", ([], T.ym[:], []), C("M", 0, 2048), 3.0,
                [lambda k=k: g.sync.dma_start(T.ym[k:k + 1, :], T.M[16 * k:16 * k + 1, 0:2048]) for k in range(8)])
        copy(IX(C("X", 2688 + 96 * t, 3520), C("ofU", 32, 48)), C("RP", 288 * t, 288 * t + 256), 256, SC)
    dma("y", "o2", ([], T.yp[:, 0:1024], []), C("P", 0, 1024), 4.0)
    dma("s", "o3", ([], T.yp[:, 1024:2048], []), C("P", 1024, 2048), 4.0)
    dma("s", "o4", ([], T.yx[:, 2976:3072], []), C("X", 2976, 3072), 2.0)
    return ops


def _edges(ops):
    hist, preds = {}, []
    for i, o in enumerate(ops):
        pr = {}

        def dep(j, wait):
            if j != i:
                pr[j] = pr.get(j, False) or wait
        for regs, wr in ((o["rd"], False), (o["wr"], True)):
            for nm, lo, hi in regs:
                bank = nm in PS
                for j, l, h, w in hist.get(nm, ()):
                    same = ops[j]["q"] == o["q"] and ops[j]["kind"] == "c" and o["kind"] == "c"
                    if bank:
                        if not same:
                            dep(j, True)
                        elif o["q"] == "p":
                            dep(j, False)
                        continue
                    if l >= hi or lo >= h or not (w or wr):
                        continue
                    dep(j, not (same and not w))
        if o["dep"] is not None:
            dep(o["dep"], True)
        for regs, wr in ((o["rd"], False), (o["wr"], True)):
            for nm, lo, hi in regs:
                hl = hist.get(nm, [])
                if nm not in PS and wr:
                    hl = [e for e in hl if not (lo <= e[1] and e[2] <= hi)]
                hist[nm] = hl + [(i, lo, hi, wr)]
        preds.append(pr)
    return preds


def _schedule(ops, preds, bias):
    n = len(ops)
    wake = OPT["wake"]
    succ = [[] for _ in range(n)]
    for i in range(n):
        for j in preds[i]:
            succ[j].append(i)
    prio = [0.0] * n
    for i in range(n - 1, -1, -1):
        m = 0.0
        for k in succ[i]:
            m = max(m, prio[k])
        prio[i] = m + ops[i]["dur"] + ops[i]["lat"] + wake
    prio = [p + bias.get(o["tag"], 0.0) for p, o in zip(prio, ops)]
    left = [len(p) for p in preds]
    start, fin, ready = [0.0] * n, [0.0] * n, [0.0] * n
    free, cand, order = {}, {}, []

    def push(i):
        r = 0.0
        for j, w in preds[i].items():
            r = max(r, fin[j] + wake if w else start[j])
        ready[i] = r
        cand.setdefault(ops[i]["q"], []).append(i)
    for i in range(n):
        if left[i] == 0:
            push(i)
    while len(order) < n:
        best = None
        for q, lst in cand.items():
            if lst:
                tq = max(0.0 if q is None else free.get(q, 0.0), min([ready[i] for i in lst]))
                if best is None or tq < best[0]:
                    best = (tq, q)
        tq, q = best
        i = max([i for i in cand[q] if ready[i] <= tq + 1e-9], key=lambda k: (prio[k], -k))
        cand[q].remove(i)
        start[i] = tq
        fin[i] = tq + ops[i]["dur"] + ops[i]["lat"]
        if q is not None:
            free[q] = tq + ops[i]["dur"]
        order.append(i)
        for k in succ[i]:
            left[k] -= 1
            if left[k] == 0:
                push(k)
    return order, start, fin


def _plan(ops):
    preds = _edges(ops)
    tags = sorted({o["tag"] for o in ops if o["tag"][0] != "s"})
    rng = np.random.default_rng(OPT["seed"])
    bias = dict(OPT["bias"])
    best = _schedule(ops, preds, bias)
    for k in range(OPT["search"]):
        b = dict(bias)
        for _ in range(int(rng.integers(1, 4))):
            tg = tags[int(rng.integers(len(tags)))]
            b[tg] = b.get(tg, 0.0) + float(rng.normal()) * (2.0, 6.0, 15.0)[int(rng.integers(3))]
        r = _schedule(ops, preds, b)
        if max(r[2]) <= max(best[2]):
            best, bias = r, b
    return (preds,) + best


def rank_program(g, core, T, topo):
    rank = T.rank_of(core)
    if rank is None:
        return
    ops = _build(g, T, topo, core, rank)
    if not ORDER:
        ORDER.append(_plan(ops))
    preds, order, start, fin = ORDER[0]
    queue = {"v": g.vector, "s": g.scalar, "p": g.tensor, "g": g, "y": g.sync}
    known = {q: {} for q in queue}
    count, token = {}, {}
    for i in order:
        o = ops[i]
        q = o["q"]
        if q is None:
            count[o["sem"]] = count.get(o["sem"], 0) + o["inc"]
            token[i] = (o["sem"], count[o["sem"]], {})
            continue
        kn = known[q]
        for j in sorted(preds[i], key=lambda j: -fin[j]):
            if not preds[i][j]:
                continue
            sem, val, snap = token[j]
            if kn.get(sem, 0) >= val:
                continue
            queue[q].wait_ge(T.sem[sem], val)
            kn[sem] = val
            for s2, v2 in snap.items():
                if kn.get(s2, 0) < v2:
                    kn[s2] = v2
        for f in o["calls"]:
            ins = f()
            if o["kind"] != "r":
                ins.then_inc(T.sem[o["sem"]], o["inc"])
            count[o["sem"]] = count.get(o["sem"], 0) + o["inc"]
        token[i] = (o["sem"], count[o["sem"]], dict(kn))
    for sem in sorted(count):
        if known["g"].get(sem, 0) < count[sem]:
            g.wait_ge(T.sem[sem], count[sem])
